import numpy as np
import ml_dtypes


def mxq(x, axis, fmt="e4m3"):
    dtype, down = {"e4m3": (ml_dtypes.float8_e4m3fn, 7), "e5m2": (ml_dtypes.float8_e5m2, 14)}[fmt]
    v = np.moveaxis(np.asarray(x, np.float32).astype(ml_dtypes.bfloat16).astype(np.float64), axis, -1)
    blocks = v.reshape(v.shape[:-1] + (-1, 32))
    amax = np.abs(blocks).max(-1, keepdims=True)
    byte = np.maximum(np.where(amax > 0, np.frexp(amax)[1] - 1 + 127, 0) - down, 1)
    scale = np.exp2(byte - 127.0)
    codes = (blocks / scale).astype(np.float32).astype(dtype).astype(np.float64)
    return np.moveaxis((codes * scale).reshape(v.shape), -1, axis)


WIDE = False


def mx_kscale(k):
    if not WIDE:
        return np.ones(k)
    levels = np.array([10, -10, 5, -5, 0])
    if k % 512:
        return np.exp2(np.random.permutation(np.resize(levels, k // 32))).repeat(32)
    a = np.empty((k // 512, 16))
    for p in range(k // 512):
        a[p, :8] = np.random.permutation(np.resize(levels, 8))
        for g in range(8):
            far = levels[np.abs(levels - a[p, g]) >= 10]
            a[p, g + 8] = far[np.random.randint(len(far))]
    return np.exp2(a.ravel()).repeat(32)


BF16 = ml_dtypes.bfloat16


def bf(x):
    return np.asarray(x, np.float32).astype(BF16)


def f64(x):
    return np.asarray(x).astype(np.float64)

def planes(Y):
    n, m = Y.shape
    b = f64(bf(Y)).reshape(n // 32, 32, m)
    amax = np.abs(b).max(1)
    byte = np.clip(np.where(amax > 0, np.frexp(amax)[1] - 1 + 127 - 7, 1), 1, 254)
    codes = (b * np.exp2(127.0 - byte)[:, None, :]).reshape(n, m).astype(np.float32).astype(ml_dtypes.float8_e4m3fn).view(np.uint8)
    words = codes.reshape(n // 512, 128, 4, m).transpose(0, 1, 3, 2)
    return np.ascontiguousarray(words), np.ascontiguousarray(byte.astype(np.uint8).reshape(n // 512, 16, m))


W, N = 2, 512


def setup_inputs():
    s, t = mx_kscale(N), mx_kscale(N)
    gu = np.random.standard_normal((W, N, N)) * 0.6
    gd = np.random.standard_normal((W, N, N))
    kf = np.random.standard_normal((N, N)) / np.sqrt(N)
    kb = np.random.standard_normal((N, N)) / np.sqrt(N)
    v = np.random.standard_normal((W, N)) * 0.5
    return {"gu": bf(gu * s[:, None] * t[None, :]), "gd": bf(gd * s[:, None] * t[None, :]),
            "kf": bf(kf / s[None, :]), "kb": bf(kb / t[:, None]), "v": bf(v)}


def wrap(a, kfq, kbq):
    left = kfq @ mxq(a, 1, "e4m3")
    return mxq(left, 2, "e4m3") @ kbq


def core(gu, gd, kf, kb, v):
    gu, gd, kf, kb, v = f64(gu), f64(gd), f64(kf), f64(kb), f64(v)
    n = gu.shape[-1]
    vi = v[:, :, None]
    vj = v[:, None, :]
    au = np.exp(vi - vj) * gu
    ad = np.exp(vj - vi) * gd
    kfq = mxq(kf, 1, "e4m3")
    kbq = mxq(kb, 0, "e4m3")
    pu = wrap(au, kfq, kbq)
    pd = wrap(ad, kfq, kbq)
    delta = np.eye(n)
    return (delta[None, :, :] - np.swapaxes(pu, -1, -2)) * pd


def reference(gu, gd, kf, kb, v):
    R_out = core(gu, gd, kf, kb, v)
    words, scales = planes(np.moveaxis(R_out, 1, 0).reshape(512, -1))
    return R_out, words, scales

@@ -1,0 +1,368 @@
+from contextlib import ExitStack
+
+import concourse.mybir as mybir
+from concourse.masks import make_identity
+
+W, N = 2, 512
+P = 128
+T = 4
+
+F32 = mybir.dt.float32
+BF16 = mybir.dt.bfloat16
+U32 = mybir.dt.uint32
+I32 = mybir.dt.int32
+U8 = mybir.dt.uint8
+FP8X4 = mybir.dt.float8_e4m3fn_x4
+EXP = mybir.ActivationFunctionType.Exp
+MULT = mybir.AluOpType.mult
+SUB = mybir.AluOpType.subtract
+
+FLOPS = W * 4 * 2 * N * N * N
+
+
+def tile_twospinpropagatorwraptransversecorrelati_x1_kernel(
+    tc, gu, gd, kf, kb, v, out_0, out_1, out_2
+):
+    nc = tc.nc
+    with ExitStack() as ctx:
+        keep = ctx.enter_context(tc.tile_pool(name="keep", bufs=1))
+        psum = ctx.enter_context(tc.psum_pool(name="psum", bufs=8))
+        ctx.enter_context(tc.manual_schedule())
+
+        chains = [(w, s) for w in range(W) for s in "ud"]
+
+        v_sb = keep.tile([P, W, T], BF16, name="v_sb")
+        nc.sync.dma_start(out=v_sb[:], in_=v.rearrange("w (p t) -> p w t", t=T))
+        g_sb = {}
+        kb_sb = keep.tile([P, T, N], BF16, name="kb_sb")
+
+        def load_g(w, s):
+            g_sb[w, s] = keep.tile([P, T, N], BF16, name=f"g_{w}{s}")
+            src = gu if s == "u" else gd
+            nc.sync.dma_start(out=g_sb[w, s][:], in_=src[w].rearrange("(p t) j -> p t j", t=T))
+
+        load_g(0, "u")
+        kf_sb = keep.tile([P, T * N], BF16, name="kf_sb")
+        for h in range(2):
+            nc.sync.dma_start(
+                out=kf_sb[:, 1024 * h : 1024 * (h + 1)].rearrange("p (t k) -> p t k", t=2),
+                in_=kf.rearrange("(p t) k -> p t k", t=T)[:, 2 * h : 2 * h + 2, :],
+            )
+        load_g(0, "d")
+        nc.sync.dma_start(out=kb_sb[:], in_=kb.rearrange("(p t) n -> p t n", t=T))
+        load_g(1, "u")
+        load_g(1, "d")
+
+        ident_b = keep.tile([P, P], BF16, name="ident_b")
+        ident_f = keep.tile([P, P], F32, name="ident_f")
+        make_identity(nc, ident_b[:])
+        make_identity(nc, ident_f[:])
+
+        v_pos = keep.tile([P, W, T], F32, name="v_pos")
+        v_neg = keep.tile([P, W, T], F32, name="v_neg")
+        nc.vector.tensor_copy(out=v_pos[:], in_=v_sb[:])
+        nc.vector.tensor_scalar(out=v_neg[:], in0=v_sb[:], scalar1=-1.0, scalar2=None, op0=MULT)
+        kf_t = []
+        for h in range(2):
+            bank = psum.tile([P, N], F32, name="bank")
+            kf_t.append(bank)
+        v_row = psum.tile([P, W * N], BF16, name="bank")
+        for w in range(W):
+            for t in range(T):
+                col = w * N + t * P
+                nc.tensor.transpose(
+                    v_row[:, col : col + P], v_sb[:, w, t : t + 1].to_broadcast([P, P]), ident_b[:]
+                )
+
+        e_sb = {}
+
+        def factors(w, s, halves):
+            if (w, s) not in e_sb:
+                e_sb[w, s] = keep.tile([P, T, N], F32, name=f"e_{w}{s}")
+            for c0, c1 in halves:
+                for t in range(T):
+                    nc.scalar.activation(
+                        out=e_sb[w, s][:, t, c0:c1],
+                        in_=v_row[:, w * N + c0 : w * N + c1],
+                        func=EXP,
+                        scale=-1.0 if s == "u" else 1.0,
+                        bias=(v_pos if s == "u" else v_neg)[:, w, t : t + 1],
+                    )
+
+        HALVES = [(0, 256), (256, 512)]
+        FULL = [(0, 512)]
+
+        kf_words = kf_sb[:].bitcast(F32)
+        kf_g = keep.tile([P, T * N], BF16, name="kf_g", align_bytes=64)
+        kf_c = keep.tile([P, N], U32, name="kf_c", align_bytes=64)
+        kf_s = keep.tile([P, N], U8, name="kf_s", align_bytes=64)
+        for h in range(2):
+            bank = kf_t[h]
+            for t2 in range(2):
+                for u in range(2):
+                    t = 2 * h + t2
+                    nc.tensor.transpose(
+                        bank[:, (2 * t2 + u) * P : (2 * t2 + u + 1) * P],
+                        kf_words[:, 256 * t + u : 256 * (t + 1) : 2],
+                        ident_f[:],
+                    )
+        def copy_kf(h, copy):
+            copy(
+                out=kf_g[:].bitcast(F32)[:, 512 * h : 512 * (h + 1)].rearrange("p (t q u) -> p t q u", t=2, u=2),
+                in_=kf_t[h][:].rearrange("p (t u q) -> p t q u", t=2, u=2),
+            )
+
+        def quant(codes, scales, grouped, c0, c1):
+            nc.vector.quantize_mx(
+                out=codes[:, c0:c1].bitcast(FP8X4),
+                scales=scales[:, c0:c1],
+                in_=grouped[:, T * c0 : T * c1],
+            )
+
+        def quant_kf():
+            for c0, c1 in HALVES:
+                quant(kf_c, kf_s, kf_g, c0, c1)
+
+        a_g, a_c, a_s = {}, {}, {}
+
+        ed = {}
+
+        def turn_factors(w):
+            ed[w] = []
+            for tj in range(T):
+                bank = psum.tile([P, N], F32, name="bank")
+                ed[w].append(bank)
+                for ti in range(T):
+                    nc.tensor.transpose(
+                        bank[:, ti * P : (ti + 1) * P], e_sb[w, "u"][:, tj, ti * P : (ti + 1) * P], ident_f[:]
+                    )
+
+        def make_a(w, s):
+            a_g[w, s] = keep.tile([P, T * N], BF16, name=f"ag_{w}{s}", align_bytes=64)
+            a_c[w, s] = keep.tile([P, N], U32, name=f"ac_{w}{s}", align_bytes=64)
+            a_s[w, s] = keep.tile([P, N], U8, name=f"as_{w}{s}", align_bytes=64)
+            if s == "u":
+                for h in range(2):
+                    nc.vector.tensor_tensor(
+                        out=a_g[w, s][:, 1024 * h : 1024 * (h + 1)].rearrange("p (t q i) -> p t q i", t=2, i=T),
+                        in0=g_sb[w, s][:].rearrange("p i (q t) -> p t q i", t=T)[:, 2 * h : 2 * h + 2, :, :],
+                        in1=e_sb[w, s][:].rearrange("p i (t q) -> p t q i", t=T)[:, 2 * h : 2 * h + 2, :, :],
+                        op=MULT,
+                    )
+            else:
+                for tj in range(T):
+                    nc.vector.tensor_tensor(
+                        out=a_g[w, s][:, N * tj : N * (tj + 1)].rearrange("p (q i) -> p q i", i=T),
+                        in0=g_sb[w, s][:].rearrange("p i (q t) -> p t q i", t=T)[:, tj, :, :],
+                        in1=ed[w][tj][:].rearrange("p (i q) -> p q i", i=T),
+                        op=MULT,
+                    )
+
+        def quant_a(w, s):
+            for c0, c1 in HALVES:
+                quant(a_c[w, s], a_s[w, s], a_g[w, s], c0, c1)
+
+        m1 = {}
+
+        def stage1(w, s):
+            banks = []
+            for tm in range(T):
+                bank = psum.tile([P, N], F32, name="bank")
+                banks.append(bank)
+            m1[w, s] = banks
+            for tm in range(T):
+                for tj in range(T):
+                    nc.tensor.matmul_mx(
+                        out=banks[tm][:, tj * P : (tj + 1) * P],
+                        lhsT=a_c[w, s][:, tj * P : (tj + 1) * P].bitcast(FP8X4),
+                        lhsT_scale=a_s[w, s][:, tj * P : (tj + 1) * P],
+                        rhs=kf_c[:, tm * P : (tm + 1) * P].bitcast(FP8X4),
+                        rhs_scale=kf_s[:, tm * P : (tm + 1) * P],
+                        start=True,
+                        stop=True,
+                    )
+
+        l_g, l_c, l_s = {}, {}, {}
+
+        def copy_l(w, s):
+            l_g[w, s] = keep.tile([P, T * N], BF16, name=f"lg_{w}{s}", align_bytes=64)
+            for tm in range(T):
+                nc.scalar.copy(
+                    out=l_g[w, s][:, tm * N : (tm + 1) * N].rearrange("p (q t) -> p q t", t=T),
+                    in_=m1[w, s][tm][:].rearrange("p (t q) -> p q t", t=T),
+                )
+
+        def quant_l(w, s):
+            l_c[w, s] = keep.tile([P, N], U32, name=f"lc_{w}{s}", align_bytes=64)
+            l_s[w, s] = keep.tile([P, N], U8, name=f"ls_{w}{s}", align_bytes=64)
+            for c0, c1 in HALVES:
+                quant(l_c[w, s], l_s[w, s], l_g[w, s], c0, c1)
+
+        kb_g = keep.tile([P, T * N], BF16, name="kb_g", align_bytes=64)
+        kb_c = keep.tile([P, N], U32, name="kb_c", align_bytes=64)
+        kb_s = keep.tile([P, N], U8, name="kb_s", align_bytes=64)
+
+        def copy_kb(h, copy):
+            copy(
+                out=kb_g[:, 1024 * h : 1024 * (h + 1)].rearrange("p (t q j) -> p t q j", t=2, j=T),
+                in_=kb_sb[:].rearrange("p j (q t) -> p t q j", t=T)[:, 2 * h : 2 * h + 2, :, :],
+            )
+
+        def quant_kb():
+            for c0, c1 in HALVES:
+                quant(kb_c, kb_s, kb_g, c0, c1)
+
+        pu, pd = {}, {}
+
+        def stage2_u(w):
+            diag = psum.tile([P, N], F32, name="bank")
+            off = []
+            for b in range(3):
+                bank = psum.tile([P, N], F32, name="bank")
+                off.append(bank)
+            pu[w] = (diag, off)
+            for ti in range(T):
+                for tj in range(T):
+                    run, pos = divmod(T * ti + tj, 5)
+                    dst = diag[:, run * P : (run + 1) * P] if pos == 0 else off[run][:, (pos - 1) * P : pos * P]
+                    nc.tensor.matmul_mx(
+                        out=dst,
+                        lhsT=kb_c[:, ti * P : (ti + 1) * P].bitcast(FP8X4),
+                        lhsT_scale=kb_s[:, ti * P : (ti + 1) * P],
+                        rhs=l_c[w, "u"][:, tj * P : (tj + 1) * P].bitcast(FP8X4),
+                        rhs_scale=l_s[w, "u"][:, tj * P : (tj + 1) * P],
+                        start=True,
+                        stop=True,
+                    )
+
+        def stage2_d(w):
+            banks = []
+            for ti in range(T):
+                bank = psum.tile([P, N], F32, name="bank")
+                banks.append(bank)
+                nc.tensor.matmul_mx(
+                    out=bank[:],
+                    lhsT=l_c[w, "d"][:, ti * P : (ti + 1) * P].bitcast(FP8X4),
+                    lhsT_scale=l_s[w, "d"][:, ti * P : (ti + 1) * P],
+                    rhs=kb_c[:].bitcast(FP8X4),
+                    rhs_scale=kb_s[:],
+                    start=True,
+                    stop=True,
+                )
+            pd[w] = banks
+
+        n_sb = {}
+
+        def minus_pu(w):
+            n_sb[w] = keep.tile([P, 2560], F32, name=f"n_{w}")
+            for b in range(3):
+                nc.scalar.mul(
+                    out=n_sb[w][:, (5 * b + 1) * P : (5 * b + 5) * P], in_=pu[w][1][b][:], mul=-1.0
+                )
+
+        def diag_pu(w):
+            nc.vector.tensor_tensor(
+                out=n_sb[w][:].rearrange("p (a b) -> p a b", b=640)[:, :, 0:P],
+                in0=ident_f[:].unsqueeze(1).to_broadcast([P, T, P]),
+                in1=pu[w][0][:].rearrange("p (a q) -> p a q", a=T),
+                op=SUB,
+            )
+
+        o_sb, o_g = {}, {}
+        w_c = keep.tile([P, W * N], U32, name="w_c", align_bytes=64)
+        w_s = keep.tile([P, W * N], U8, name="w_s", align_bytes=64)
+
+        def product(w, h):
+            if h == 0:
+                o_sb[w] = keep.tile([P, T, N], F32, name=f"o_{w}")
+                o_g[w] = keep.tile([P, T * N], BF16, name=f"og_{w}", align_bytes=64)
+            dst = out_0[w].rearrange("(p t) n -> p t n", t=T)
+            cols = slice(256 * h, 256 * (h + 1))
+            qs = slice(64 * h, 64 * (h + 1))
+            for ti in range(T):
+                nc.vector.tensor_tensor(
+                    out=o_sb[w][:, ti, cols].rearrange("p (q t) -> p q t", t=T),
+                    in0=pd[w][ti][:].rearrange("p (t q) -> p q t", t=T)[:, qs, :],
+                    in1=n_sb[w][:, ti * N : (ti + 1) * N].rearrange("p (t q) -> p q t", t=T)[:, qs, :],
+                    op=MULT,
+                )
+            nc.sync.dma_start(out=dst[:, :, cols], in_=o_sb[w][:, :, cols])
+
+        def planes_copy(w, h, copy):
+            copy(
+                out=o_g[w][:, 1024 * h : 1024 * (h + 1)].rearrange("p (n t) -> p n t", t=T),
+                in_=o_sb[w][:, :, 256 * h : 256 * (h + 1)].rearrange("p t n -> p n t"),
+            )
+
+        def planes_quant(w, h):
+            cols = slice(w * N + 256 * h, w * N + 256 * (h + 1))
+            nc.vector.quantize_mx(
+                out=w_c[:, cols].bitcast(FP8X4),
+                scales=w_s[:, cols],
+                in_=o_g[w][:, 1024 * h : 1024 * (h + 1)],
+            )
+
+        def store_words(w):
+            nc.sync.dma_start(
+                out=out_1[0].rearrange("p m t -> p (m t)").bitcast(I32)[:, w * N : (w + 1) * N],
+                in_=w_c[:, w * N : (w + 1) * N].bitcast(I32),
+            )
+
+        vcopy, scopy = nc.vector.tensor_copy, nc.scalar.copy
+        factors(0, "u", HALVES)
+        copy_kf(0, scopy)
+        copy_kf(1, scopy)
+        make_a(0, "u")
+        turn_factors(0)
+        quant_a(0, "u")
+        quant_kf()
+        factors(1, "u", FULL)
+        stage1(0, "u")
+        make_a(0, "d")
+        copy_kb(0, scopy)
+        quant_a(0, "d")
+        stage1(0, "d")
+        copy_l(0, "u")
+        turn_factors(1)
+        make_a(1, "u")
+        quant_a(1, "u")
+        copy_l(0, "d")
+        stage1(1, "u")
+        make_a(1, "d")
+        quant_a(1, "d")
+        copy_l(1, "u")
+        stage1(1, "d")
+        copy_kb(1, vcopy)
+        quant_l(0, "u")
+        quant_kb()
+        stage2_u(0)
+        quant_l(0, "d")
+        copy_l(1, "d")
+        minus_pu(0)
+        stage2_d(0)
+        quant_l(1, "u")
+        diag_pu(0)
+        stage2_u(1)
+        minus_pu(1)
+        quant_l(1, "d")
+        product(0, 0)
+        product(0, 1)
+        diag_pu(1)
+        stage2_d(1)
+        planes_copy(0, 0, scopy)
+        planes_copy(0, 1, scopy)
+        product(1, 0)
+        planes_quant(0, 0)
+        product(1, 1)
+        planes_copy(1, 0, scopy)
+        planes_quant(0, 1)
+        store_words(0)
+        planes_copy(1, 1, vcopy)
+        planes_quant(1, 0)
+        planes_quant(1, 1)
+        store_words(1)
+        for quad in range(4):
+            nc.scalar.dma_start(
+                out=out_2[0].bitcast(I32)[4 * quad : 4 * quad + 4, :],
+                in_=w_s[32 * quad : 32 * quad + 4, :].bitcast(I32),
+            )

@@ -141,22 +141,17 @@ def tile_twospinpropagatorwraptransversecorrelati_x1_kernel(
             a_g[w, s] = keep.tile([P, T * N], BF16, name=f"ag_{w}{s}", align_bytes=64)
             a_c[w, s] = keep.tile([P, N], U32, name=f"ac_{w}{s}", align_bytes=64)
             a_s[w, s] = keep.tile([P, N], U8, name=f"as_{w}{s}", align_bytes=64)
-            if s == "u":
-                for h in range(2):
-                    nc.vector.tensor_tensor(
-                        out=a_g[w, s][:, 1024 * h : 1024 * (h + 1)].rearrange("p (t q i) -> p t q i", t=2, i=T),
-                        in0=g_sb[w, s][:].rearrange("p i (q t) -> p t q i", t=T)[:, 2 * h : 2 * h + 2, :, :],
-                        in1=e_sb[w, s][:].rearrange("p i (t q) -> p t q i", t=T)[:, 2 * h : 2 * h + 2, :, :],
-                        op=MULT,
-                    )
-            else:
-                for tj in range(T):
-                    nc.vector.tensor_tensor(
-                        out=a_g[w, s][:, N * tj : N * (tj + 1)].rearrange("p (q i) -> p q i", i=T),
-                        in0=g_sb[w, s][:].rearrange("p i (q t) -> p t q i", t=T)[:, tj, :, :],
-                        in1=ed[w][tj][:].rearrange("p (i q) -> p q i", i=T),
-                        op=MULT,
-                    )
+            for tj in range(T):
+                if s == "u":
+                    factor = e_sb[w, s][:, :, tj * P : (tj + 1) * P].rearrange("p i (b q) -> p b i q", q=4)
+                else:
+                    factor = ed[w][tj][:].rearrange("p (i b q) -> p b i q", i=T, q=4)
+                nc.vector.tensor_tensor(
+                    out=a_g[w, s][:, N * tj : N * (tj + 1)].rearrange("p (b q i) -> p b i q", q=4, i=T),
+                    in0=g_sb[w, s][:].rearrange("p i (b q t) -> p t b i q", q=4, t=T)[:, tj, :, :, :],
+                    in1=factor,
+                    op=MULT,
+                )
 
         def quant_a(w, s):
             for c0, c1 in HALVES:
@@ -203,10 +198,11 @@ def tile_twospinpropagatorwraptransversecorrelati_x1_kernel(
         kb_s = keep.tile([P, N], U8, name="kb_s", align_bytes=64)
 
         def copy_kb(h, copy):
-            copy(
-                out=kb_g[:, 1024 * h : 1024 * (h + 1)].rearrange("p (t q j) -> p t q j", t=2, j=T),
-                in_=kb_sb[:].rearrange("p j (q t) -> p t q j", t=T)[:, 2 * h : 2 * h + 2, :, :],
-            )
+            for tj in (2 * h, 2 * h + 1):
+                copy(
+                    out=kb_g[:, N * tj : N * (tj + 1)].rearrange("p (b q j) -> p b j q", q=4, j=T),
+                    in_=kb_sb[:].rearrange("p j (b q t) -> p t b j q", q=4, t=T)[:, tj, :, :, :],
+                )
 
         def quant_kb():
             for c0, c1 in HALVES:
@@ -278,20 +274,20 @@ def tile_twospinpropagatorwraptransversecorrelati_x1_kernel(
                 o_g[w] = keep.tile([P, T * N], BF16, name=f"og_{w}", align_bytes=64)
             dst = out_0[w].rearrange("(p t) n -> p t n", t=T)
             cols = slice(256 * h, 256 * (h + 1))
-            qs = slice(64 * h, 64 * (h + 1))
+            qs = slice(32 * h, 32 * (h + 1))
             for ti in range(T):
                 nc.vector.tensor_tensor(
-                    out=o_sb[w][:, ti, cols].rearrange("p (q t) -> p q t", t=T),
-                    in0=pd[w][ti][:].rearrange("p (t q) -> p q t", t=T)[:, qs, :],
-                    in1=n_sb[w][:, ti * N : (ti + 1) * N].rearrange("p (t q) -> p q t", t=T)[:, qs, :],
+                    out=o_sb[w][:, ti, cols].rearrange("p (b q t) -> p b t q", q=2, t=T),
+                    in0=pd[w][ti][:].rearrange("p (t b q) -> p b t q", t=T, q=2)[:, qs, :, :],
+                    in1=n_sb[w][:, ti * N : (ti + 1) * N].rearrange("p (t b q) -> p b t q", t=T, q=2)[:, qs, :, :],
                     op=MULT,
                 )
             nc.sync.dma_start(out=dst[:, :, cols], in_=o_sb[w][:, :, cols])
 
         def planes_copy(w, h, copy):
             copy(
-                out=o_g[w][:, 1024 * h : 1024 * (h + 1)].rearrange("p (n t) -> p n t", t=T),
-                in_=o_sb[w][:, :, 256 * h : 256 * (h + 1)].rearrange("p t n -> p n t"),
+                out=o_g[w][:, 1024 * h : 1024 * (h + 1)].rearrange("p (b n t) -> p b t n", n=4, t=T),
+                in_=o_sb[w][:, :, 256 * h : 256 * (h + 1)].rearrange("p t (b n) -> p b t n", n=4),
             )
 
         def planes_quant(w, h):

@@ -274,12 +274,12 @@ def tile_twospinpropagatorwraptransversecorrelati_x1_kernel(
                 o_g[w] = keep.tile([P, T * N], BF16, name=f"og_{w}", align_bytes=64)
             dst = out_0[w].rearrange("(p t) n -> p t n", t=T)
             cols = slice(256 * h, 256 * (h + 1))
-            qs = slice(32 * h, 32 * (h + 1))
+            qs = slice(64 * h, 64 * (h + 1))
             for ti in range(T):
                 nc.vector.tensor_tensor(
-                    out=o_sb[w][:, ti, cols].rearrange("p (b q t) -> p b t q", q=2, t=T),
-                    in0=pd[w][ti][:].rearrange("p (t b q) -> p b t q", t=T, q=2)[:, qs, :, :],
-                    in1=n_sb[w][:, ti * N : (ti + 1) * N].rearrange("p (t b q) -> p b t q", t=T, q=2)[:, qs, :, :],
+                    out=o_sb[w][:, ti, cols].rearrange("p (q t) -> p q t", t=T),
+                    in0=pd[w][ti][:].rearrange("p (t q) -> p q t", t=T)[:, qs, :],
+                    in1=n_sb[w][:, ti * N : (ti + 1) * N].rearrange("p (t q) -> p q t", t=T)[:, qs, :],
                     op=MULT,
                 )
             nc.sync.dma_start(out=dst[:, :, cols], in_=o_sb[w][:, :, cols])

@@ -26,7 +26,8 @@ def tile_twospinpropagatorwraptransversecorrelati_x1_kernel(
     nc = tc.nc
     with ExitStack() as ctx:
         keep = ctx.enter_context(tc.tile_pool(name="keep", bufs=1))
-        psum = ctx.enter_context(tc.psum_pool(name="psum", bufs=8))
+        psum = ctx.enter_context(tc.psum_pool(name="psum", bufs=7))
+        warm_pool = ctx.enter_context(tc.psum_pool(name="warm_pool", bufs=1))
         ctx.enter_context(tc.manual_schedule())
 
         chains = [(w, s) for w in range(W) for s in "ud"]
@@ -67,7 +68,8 @@ def tile_twospinpropagatorwraptransversecorrelati_x1_kernel(
             bank = psum.tile([P, N], F32, name="bank")
             kf_t.append(bank)
         v_row = psum.tile([P, W * N], BF16, name="bank")
-        for w in range(W):
+
+        def spread_v(w):
             for t in range(T):
                 col = w * N + t * P
                 nc.tensor.transpose(
@@ -96,16 +98,17 @@ def tile_twospinpropagatorwraptransversecorrelati_x1_kernel(
         kf_g = keep.tile([P, T * N], BF16, name="kf_g", align_bytes=64)
         kf_c = keep.tile([P, N], U32, name="kf_c", align_bytes=64)
         kf_s = keep.tile([P, N], U8, name="kf_s", align_bytes=64)
-        for h in range(2):
-            bank = kf_t[h]
-            for t2 in range(2):
-                for u in range(2):
-                    t = 2 * h + t2
-                    nc.tensor.transpose(
-                        bank[:, (2 * t2 + u) * P : (2 * t2 + u + 1) * P],
-                        kf_words[:, 256 * t + u : 256 * (t + 1) : 2],
-                        ident_f[:],
-                    )
+        def turn_kf():
+            for h in range(2):
+                bank = kf_t[h]
+                for t2 in range(2):
+                    for u in range(2):
+                        t = 2 * h + t2
+                        nc.tensor.transpose(
+                            bank[:, (2 * t2 + u) * P : (2 * t2 + u + 1) * P],
+                            kf_words[:, 256 * t + u : 256 * (t + 1) : 2],
+                            ident_f[:],
+                        )
         def copy_kf(h, copy):
             copy(
                 out=kf_g[:].bitcast(F32)[:, 512 * h : 512 * (h + 1)].rearrange("p (t q u) -> p t q u", t=2, u=2),
@@ -156,6 +159,20 @@ def tile_twospinpropagatorwraptransversecorrelati_x1_kernel(
         def quant_a(w, s):
             for c0, c1 in HALVES:
                 quant(a_c[w, s], a_s[w, s], a_g[w, s], c0, c1)
+
+        warm_bank = warm_pool.tile([P, N], F32, name="warm_bank")
+
+        def warm(n):
+            for i in range(n):
+                nc.tensor.matmul_mx(
+                    out=warm_bank[:],
+                    lhsT=kf_c[:, 0:P].bitcast(FP8X4),
+                    lhsT_scale=kf_s[:, 0:P],
+                    rhs=kf_c[:].bitcast(FP8X4),
+                    rhs_scale=kf_s[:],
+                    start=True,
+                    stop=True,
+                )
 
         m1 = {}
 
@@ -298,36 +315,44 @@ def tile_twospinpropagatorwraptransversecorrelati_x1_kernel(
                 in_=o_g[w][:, 1024 * h : 1024 * (h + 1)],
             )
 
-        def store_words(w):
+        def store_words(c0, c1):
             nc.sync.dma_start(
-                out=out_1[0].rearrange("p m t -> p (m t)").bitcast(I32)[:, w * N : (w + 1) * N],
-                in_=w_c[:, w * N : (w + 1) * N].bitcast(I32),
+                out=out_1[0].rearrange("p m t -> p (m t)").bitcast(I32)[:, c0:c1],
+                in_=w_c[:, c0:c1].bitcast(I32),
             )
 
         vcopy, scopy = nc.vector.tensor_copy, nc.scalar.copy
+        spread_v(0)
+        turn_kf()
         factors(0, "u", HALVES)
         copy_kf(0, scopy)
         copy_kf(1, scopy)
         make_a(0, "u")
+        spread_v(1)
         turn_factors(0)
-        quant_a(0, "u")
         quant_kf()
+        quant_a(0, "u")
         factors(1, "u", FULL)
+        warm(1)
         stage1(0, "u")
+        warm(2)
         make_a(0, "d")
         copy_kb(0, scopy)
         quant_a(0, "d")
         stage1(0, "d")
         copy_l(0, "u")
         turn_factors(1)
+        warm(2)
         make_a(1, "u")
         quant_a(1, "u")
         copy_l(0, "d")
         stage1(1, "u")
+        warm(2)
         make_a(1, "d")
         quant_a(1, "d")
         copy_l(1, "u")
         stage1(1, "d")
+        warm(1)
         copy_kb(1, vcopy)
         quant_l(0, "u")
         quant_kb()
@@ -352,13 +377,15 @@ def tile_twospinpropagatorwraptransversecorrelati_x1_kernel(
         product(1, 1)
         planes_copy(1, 0, scopy)
         planes_quant(0, 1)
-        store_words(0)
+        store_words(0, 512)
         planes_copy(1, 1, vcopy)
         planes_quant(1, 0)
+        store_words(512, 768)
         planes_quant(1, 1)
-        store_words(1)
+        store_words(768, 1024)
         for quad in range(4):
-            nc.scalar.dma_start(
+            queue = nc.scalar if quad < 2 else nc.sync
+            queue.dma_start(
                 out=out_2[0].bitcast(I32)[4 * quad : 4 * quad + 4, :],
                 in_=w_s[32 * quad : 32 * quad + 4, :].bitcast(I32),
             )

@@ -26,11 +26,16 @@ def tile_twospinpropagatorwraptransversecorrelati_x1_kernel(
     nc = tc.nc
     with ExitStack() as ctx:
         keep = ctx.enter_context(tc.tile_pool(name="keep", bufs=1))
-        psum = ctx.enter_context(tc.psum_pool(name="psum", bufs=7))
-        warm_pool = ctx.enter_context(tc.psum_pool(name="warm_pool", bufs=1))
+        px = ctx.enter_context(tc.psum_pool(name="px", bufs=4))
+        py = ctx.enter_context(tc.psum_pool(name="py", bufs=4))
         ctx.enter_context(tc.manual_schedule())
 
         chains = [(w, s) for w in range(W) for s in "ud"]
+
+        zero = keep.tile([P, 1], F32, name="zero")
+        one = keep.tile([P, 1], F32, name="one")
+        nc.vector.memset(zero[:], 0.0)
+        nc.scalar.activation(out=one[:], in_=zero[:], func=EXP)
 
         v_sb = keep.tile([P, W, T], BF16, name="v_sb")
         nc.sync.dma_start(out=v_sb[:], in_=v.rearrange("w (p t) -> p w t", t=T))
@@ -60,14 +65,12 @@ def tile_twospinpropagatorwraptransversecorrelati_x1_kernel(
         make_identity(nc, ident_f[:])
 
         v_pos = keep.tile([P, W, T], F32, name="v_pos")
-        v_neg = keep.tile([P, W, T], F32, name="v_neg")
         nc.vector.tensor_copy(out=v_pos[:], in_=v_sb[:])
-        nc.vector.tensor_scalar(out=v_neg[:], in0=v_sb[:], scalar1=-1.0, scalar2=None, op0=MULT)
         kf_t = []
         for h in range(2):
-            bank = psum.tile([P, N], F32, name="bank")
+            bank = px.tile([P, N], F32, name="bank")
             kf_t.append(bank)
-        v_row = psum.tile([P, W * N], BF16, name="bank")
+        v_row = px.tile([P, W * N], BF16, name="bank")
 
         def spread_v(w):
             for t in range(T):
@@ -78,18 +81,25 @@ def tile_twospinpropagatorwraptransversecorrelati_x1_kernel(
 
         e_sb = {}
 
-        def factors(w, s, halves):
-            if (w, s) not in e_sb:
-                e_sb[w, s] = keep.tile([P, T, N], F32, name=f"e_{w}{s}")
-            for c0, c1 in halves:
+        def factors(w, halves):
+            step = N // halves
+            e_sb[w] = []
+            for h in range(halves):
+                part = keep.tile([P, T, step], F32, name=f"e_{w}{h}")
+                e_sb[w].append(part)
                 for t in range(T):
                     nc.scalar.activation(
-                        out=e_sb[w, s][:, t, c0:c1],
-                        in_=v_row[:, w * N + c0 : w * N + c1],
+                        out=part[:, t, :],
+                        in_=v_row[:, w * N + h * step : w * N + (h + 1) * step],
                         func=EXP,
-                        scale=-1.0 if s == "u" else 1.0,
-                        bias=(v_pos if s == "u" else v_neg)[:, w, t : t + 1],
+                        scale=-1.0,
+                        bias=v_pos[:, w, t : t + 1],
                     )
+
+        def factor_cols(w, t):
+            parts = e_sb[w]
+            per = T // len(parts)
+            return parts[t // per][:, :, (t % per) * P : (t % per + 1) * P]
 
         HALVES = [(0, 256), (256, 512)]
         FULL = [(0, 512)]
@@ -132,12 +142,13 @@ def tile_twospinpropagatorwraptransversecorrelati_x1_kernel(
 
         def turn_factors(w):
             ed[w] = []
+            psum = (py, px)[w]
             for tj in range(T):
                 bank = psum.tile([P, N], F32, name="bank")
                 ed[w].append(bank)
                 for ti in range(T):
                     nc.tensor.transpose(
-                        bank[:, ti * P : (ti + 1) * P], e_sb[w, "u"][:, tj, ti * P : (ti + 1) * P], ident_f[:]
+                        bank[:, ti * P : (ti + 1) * P], factor_cols(w, ti)[:, tj, :], ident_f[:]
                     )
 
         def make_a(w, s):
@@ -146,7 +157,7 @@ def tile_twospinpropagatorwraptransversecorrelati_x1_kernel(
             a_s[w, s] = keep.tile([P, N], U8, name=f"as_{w}{s}", align_bytes=64)
             for tj in range(T):
                 if s == "u":
-                    factor = e_sb[w, s][:, :, tj * P : (tj + 1) * P].rearrange("p i (b q) -> p b i q", q=4)
+                    factor = factor_cols(w, tj).rearrange("p i (b q) -> p b i q", q=4)
                 else:
                     factor = ed[w][tj][:].rearrange("p (i b q) -> p b i q", i=T, q=4)
                 nc.vector.tensor_tensor(
@@ -160,24 +171,11 @@ def tile_twospinpropagatorwraptransversecorrelati_x1_kernel(
             for c0, c1 in HALVES:
                 quant(a_c[w, s], a_s[w, s], a_g[w, s], c0, c1)
 
-        warm_bank = warm_pool.tile([P, N], F32, name="warm_bank")
-
-        def warm(n):
-            for i in range(n):
-                nc.tensor.matmul_mx(
-                    out=warm_bank[:],
-                    lhsT=kf_c[:, 0:P].bitcast(FP8X4),
-                    lhsT_scale=kf_s[:, 0:P],
-                    rhs=kf_c[:].bitcast(FP8X4),
-                    rhs_scale=kf_s[:],
-                    start=True,
-                    stop=True,
-                )
-
         m1 = {}
 
         def stage1(w, s):
             banks = []
+            psum = {"0u": px, "0d": py, "1u": py, "1d": px}[f"{w}{s}"]
             for tm in range(T):
                 bank = psum.tile([P, N], F32, name="bank")
                 banks.append(bank)
@@ -228,28 +226,29 @@ def tile_twospinpropagatorwraptransversecorrelati_x1_kernel(
         pu, pd = {}, {}
 
         def stage2_u(w):
-            diag = psum.tile([P, N], F32, name="bank")
-            off = []
-            for b in range(3):
-                bank = psum.tile([P, N], F32, name="bank")
-                off.append(bank)
-            pu[w] = (diag, off)
+            pu[w] = {}
+            psum = (py, px)[w]
+            for t2 in range(2):
+                for far in range(2):
+                    bank = psum.tile([P, N], F32, name="bank")
+                    pu[w][t2, far] = bank
             for ti in range(T):
-                for tj in range(T):
-                    run, pos = divmod(T * ti + tj, 5)
-                    dst = diag[:, run * P : (run + 1) * P] if pos == 0 else off[run][:, (pos - 1) * P : pos * P]
+                for far in range(2):
+                    half = (ti // 2) ^ far
+                    cols = slice(2 * half * P, 2 * (half + 1) * P)
                     nc.tensor.matmul_mx(
-                        out=dst,
+                        out=pu[w][ti // 2, far][:, (ti % 2) * 2 * P : (ti % 2 + 1) * 2 * P],
                         lhsT=kb_c[:, ti * P : (ti + 1) * P].bitcast(FP8X4),
                         lhsT_scale=kb_s[:, ti * P : (ti + 1) * P],
-                        rhs=l_c[w, "u"][:, tj * P : (tj + 1) * P].bitcast(FP8X4),
-                        rhs_scale=l_s[w, "u"][:, tj * P : (tj + 1) * P],
+                        rhs=l_c[w, "u"][:, cols].bitcast(FP8X4),
+                        rhs_scale=l_s[w, "u"][:, cols],
                         start=True,
                         stop=True,
                     )
 
         def stage2_d(w):
             banks = []
+            psum = (py, px)[w]
             for ti in range(T):
                 bank = psum.tile([P, N], F32, name="bank")
                 banks.append(bank)
@@ -264,22 +263,38 @@ def tile_twospinpropagatorwraptransversecorrelati_x1_kernel(
                 )
             pd[w] = banks
 
+
+        mask = keep.tile([P, 2, P, 2], F32, name="mask")
+        nc.gpsimd.memset(mask[:], 0.0)
+        for r in range(2):
+            nc.gpsimd.tensor_copy(out=mask[:, r, :, r], in_=ident_f[:])
+
         n_sb = {}
+        for w in range(W):
+            part = keep.tile([P, T, N], F32, name=f"n_{w}")
+            n_sb[w] = part
+
+        def n_half(w, pair, half):
+            return n_sb[w][:, 2 * pair : 2 * pair + 2, 2 * P * half : 2 * P * (half + 1)].rearrange(
+                "p r (q t) -> p r q t", t=2
+            )
 
         def minus_pu(w):
-            n_sb[w] = keep.tile([P, 2560], F32, name=f"n_{w}")
-            for b in range(3):
+            for pair in range(2):
                 nc.scalar.mul(
-                    out=n_sb[w][:, (5 * b + 1) * P : (5 * b + 5) * P], in_=pu[w][1][b][:], mul=-1.0
+                    out=n_half(w, pair, 1 - pair),
+                    in_=pu[w][pair, 1][:].rearrange("p (r t q) -> p r q t", r=2, t=2),
+                    mul=-1.0,
                 )
 
         def diag_pu(w):
-            nc.vector.tensor_tensor(
-                out=n_sb[w][:].rearrange("p (a b) -> p a b", b=640)[:, :, 0:P],
-                in0=ident_f[:].unsqueeze(1).to_broadcast([P, T, P]),
-                in1=pu[w][0][:].rearrange("p (a q) -> p a q", a=T),
-                op=SUB,
-            )
+            for pair in range(2):
+                nc.vector.tensor_tensor(
+                    out=n_half(w, pair, pair),
+                    in0=mask[:],
+                    in1=pu[w][pair, 0][:].rearrange("p (r t q) -> p r q t", r=2, t=2),
+                    op=SUB,
+                )
 
         o_sb, o_g = {}, {}
         w_c = keep.tile([P, W * N], U32, name="w_c", align_bytes=64)
@@ -287,24 +302,24 @@ def tile_twospinpropagatorwraptransversecorrelati_x1_kernel(
 
         def product(w, h):
             if h == 0:
-                o_sb[w] = keep.tile([P, T, N], F32, name=f"o_{w}")
                 o_g[w] = keep.tile([P, T * N], BF16, name=f"og_{w}", align_bytes=64)
             dst = out_0[w].rearrange("(p t) n -> p t n", t=T)
             cols = slice(256 * h, 256 * (h + 1))
+            o_sb[w, h] = keep.tile([P, T, 256], F32, name=f"o_{w}{h}")
             qs = slice(64 * h, 64 * (h + 1))
             for ti in range(T):
                 nc.vector.tensor_tensor(
-                    out=o_sb[w][:, ti, cols].rearrange("p (q t) -> p q t", t=T),
-                    in0=pd[w][ti][:].rearrange("p (t q) -> p q t", t=T)[:, qs, :],
-                    in1=n_sb[w][:, ti * N : (ti + 1) * N].rearrange("p (t q) -> p q t", t=T)[:, qs, :],
+                    out=o_sb[w, h][:, ti, :].rearrange("p (q a b) -> p q a b", a=2, b=2),
+                    in0=pd[w][ti][:].rearrange("p (a b q) -> p q a b", a=2, b=2)[:, qs, :, :],
+                    in1=n_sb[w][:, ti, :].rearrange("p (a q b) -> p q a b", a=2, b=2)[:, qs, :, :],
                     op=MULT,
                 )
-            nc.sync.dma_start(out=dst[:, :, cols], in_=o_sb[w][:, :, cols])
+            nc.sync.dma_start(out=dst[:, :, cols], in_=o_sb[w, h][:])
 
-        def planes_copy(w, h, copy):
+        def planes_copy(w, h, copy, c0=0, c1=256):
             copy(
-                out=o_g[w][:, 1024 * h : 1024 * (h + 1)].rearrange("p (b n t) -> p b t n", n=4, t=T),
-                in_=o_sb[w][:, :, 256 * h : 256 * (h + 1)].rearrange("p t (b n) -> p b t n", n=4),
+                out=o_g[w][:, 1024 * h + T * c0 : 1024 * h + T * c1].rearrange("p (b n t) -> p b t n", n=4, t=T),
+                in_=o_sb[w, h][:, :, c0:c1].rearrange("p t (b n) -> p b t n", n=4),
             )
 
         def planes_quant(w, h):
@@ -324,52 +339,47 @@ def tile_twospinpropagatorwraptransversecorrelati_x1_kernel(
         vcopy, scopy = nc.vector.tensor_copy, nc.scalar.copy
         spread_v(0)
         turn_kf()
-        factors(0, "u", HALVES)
+        factors(0, 4)
         copy_kf(0, scopy)
         copy_kf(1, scopy)
         make_a(0, "u")
         spread_v(1)
         turn_factors(0)
-        quant_kf()
         quant_a(0, "u")
-        factors(1, "u", FULL)
-        warm(1)
+        quant_kf()
+        factors(1, 1)
         stage1(0, "u")
-        warm(2)
         make_a(0, "d")
         copy_kb(0, scopy)
+        copy_kb(1, scopy)
         quant_a(0, "d")
         stage1(0, "d")
         copy_l(0, "u")
         turn_factors(1)
-        warm(2)
         make_a(1, "u")
         quant_a(1, "u")
         copy_l(0, "d")
         stage1(1, "u")
-        warm(2)
         make_a(1, "d")
         quant_a(1, "d")
         copy_l(1, "u")
         stage1(1, "d")
-        warm(1)
-        copy_kb(1, vcopy)
-        quant_l(0, "u")
         quant_kb()
+        quant_l(0, "u")
         stage2_u(0)
         quant_l(0, "d")
-        copy_l(1, "d")
-        minus_pu(0)
         stage2_d(0)
+        minus_pu(0)
+        copy_l(1, "d")
         quant_l(1, "u")
-        diag_pu(0)
         stage2_u(1)
-        minus_pu(1)
-        quant_l(1, "d")
+        diag_pu(0)
         product(0, 0)
         product(0, 1)
-        diag_pu(1)
+        quant_l(1, "d")
         stage2_d(1)
+        diag_pu(1)
+        minus_pu(1)
         planes_copy(0, 0, scopy)
         planes_copy(0, 1, scopy)
         product(1, 0)
@@ -378,7 +388,8 @@ def tile_twospinpropagatorwraptransversecorrelati_x1_kernel(
         planes_copy(1, 0, scopy)
         planes_quant(0, 1)
         store_words(0, 512)
-        planes_copy(1, 1, vcopy)
+        planes_copy(1, 1, vcopy, 0, 160)
+        planes_copy(1, 1, scopy, 160, 256)
         planes_quant(1, 0)
         store_words(512, 768)
         planes_quant(1, 1)

from contextlib import ExitStack

import concourse.mybir as mybir
from concourse.masks import make_identity

W, N = 2, 512
P = 128
T = 4

F32 = mybir.dt.float32
BF16 = mybir.dt.bfloat16
U32 = mybir.dt.uint32
I32 = mybir.dt.int32
U8 = mybir.dt.uint8
FP8X4 = mybir.dt.float8_e4m3fn_x4
EXP = mybir.ActivationFunctionType.Exp
MULT = mybir.AluOpType.mult
SUB = mybir.AluOpType.subtract

FLOPS = W * 4 * 2 * N * N * N


def tile_twospinpropagatorwraptransversecorrelati_x1_kernel(
    tc, gu, gd, kf, kb, v, out_0, out_1, out_2
):
    nc = tc.nc
    with ExitStack() as ctx:
        keep = ctx.enter_context(tc.tile_pool(name="keep", bufs=1))
        px = ctx.enter_context(tc.psum_pool(name="px", bufs=4))
        py = ctx.enter_context(tc.psum_pool(name="py", bufs=4))
        ctx.enter_context(tc.manual_schedule())

        chains = [(w, s) for w in range(W) for s in "ud"]

        zero = keep.tile([P, 1], F32, name="zero")
        one = keep.tile([P, 1], F32, name="one")
        nc.vector.memset(zero[:], 0.0)
        nc.scalar.activation(out=one[:], in_=zero[:], func=EXP)

        v_sb = keep.tile([P, W, T], BF16, name="v_sb")
        nc.sync.dma_start(out=v_sb[:], in_=v.rearrange("w (p t) -> p w t", t=T))
        g_sb = {}
        kb_sb = keep.tile([P, T, N], BF16, name="kb_sb")

        def load_g(w, s):
            g_sb[w, s] = keep.tile([P, T, N], BF16, name=f"g_{w}{s}")
            src = gu if s == "u" else gd
            nc.sync.dma_start(out=g_sb[w, s][:], in_=src[w].rearrange("(p t) j -> p t j", t=T))

        load_g(0, "u")
        kf_sb = keep.tile([P, T * N], BF16, name="kf_sb")
        for h in range(2):
            nc.sync.dma_start(
                out=kf_sb[:, 1024 * h : 1024 * (h + 1)].rearrange("p (t k) -> p t k", t=2),
                in_=kf.rearrange("(p t) k -> p t k", t=T)[:, 2 * h : 2 * h + 2, :],
            )
        load_g(0, "d")
        nc.sync.dma_start(out=kb_sb[:], in_=kb.rearrange("(p t) n -> p t n", t=T))
        load_g(1, "u")
        load_g(1, "d")

        ident_b = keep.tile([P, P], BF16, name="ident_b")
        ident_f = keep.tile([P, P], F32, name="ident_f")
        make_identity(nc, ident_b[:])
        make_identity(nc, ident_f[:])

        v_pos = keep.tile([P, W, T], F32, name="v_pos")
        nc.vector.tensor_copy(out=v_pos[:], in_=v_sb[:])
        kf_t = []
        for h in range(2):
            bank = px.tile([P, N], F32, name="bank")
            kf_t.append(bank)
        v_row = px.tile([P, W * N], BF16, name="bank")

        def spread_v(w):
            for t in range(T):
                col = w * N + t * P
                nc.tensor.transpose(
                    v_row[:, col : col + P], v_sb[:, w, t : t + 1].to_broadcast([P, P]), ident_b[:]
                )

        e_sb = {}

        def factors(w, halves):
            step = N // halves
            e_sb[w] = []
            for h in range(halves):
                part = keep.tile([P, T, step], F32, name=f"e_{w}{h}")
                e_sb[w].append(part)
                for t in range(T):
                    nc.scalar.activation(
                        out=part[:, t, :],
                        in_=v_row[:, w * N + h * step : w * N + (h + 1) * step],
                        func=EXP,
                        scale=-1.0,
                        bias=v_pos[:, w, t : t + 1],
                    )

        def factor_cols(w, t):
            parts = e_sb[w]
            per = T // len(parts)
            return parts[t // per][:, :, (t % per) * P : (t % per + 1) * P]

        HALVES = [(0, 256), (256, 512)]
        FULL = [(0, 512)]

        kf_words = kf_sb[:].bitcast(F32)
        kf_g = keep.tile([P, T * N], BF16, name="kf_g", align_bytes=64)
        kf_c = keep.tile([P, N], U32, name="kf_c", align_bytes=64)
        kf_s = keep.tile([P, N], U8, name="kf_s", align_bytes=64)
        def turn_kf():
            for h in range(2):
                bank = kf_t[h]
                for t2 in range(2):
                    for u in range(2):
                        t = 2 * h + t2
                        nc.tensor.transpose(
                            bank[:, (2 * t2 + u) * P : (2 * t2 + u + 1) * P],
                            kf_words[:, 256 * t + u : 256 * (t + 1) : 2],
                            ident_f[:],
                        )
        def copy_kf(h, copy):
            copy(
                out=kf_g[:].bitcast(F32)[:, 512 * h : 512 * (h + 1)].rearrange("p (t q u) -> p t q u", t=2, u=2),
                in_=kf_t[h][:].rearrange("p (t u q) -> p t q u", t=2, u=2),
            )

        def quant(codes, scales, grouped, c0, c1):
            nc.vector.quantize_mx(
                out=codes[:, c0:c1].bitcast(FP8X4),
                scales=scales[:, c0:c1],
                in_=grouped[:, T * c0 : T * c1],
            )

        def quant_kf():
            for c0, c1 in HALVES:
                quant(kf_c, kf_s, kf_g, c0, c1)

        a_g, a_c, a_s = {}, {}, {}

        ed = {}

        def turn_factors(w):
            ed[w] = []
            psum = (py, px)[w]
            for tj in range(T):
                bank = psum.tile([P, N], F32, name="bank")
                ed[w].append(bank)
                for ti in range(T):
                    nc.tensor.transpose(
                        bank[:, ti * P : (ti + 1) * P], factor_cols(w, ti)[:, tj, :], ident_f[:]
                    )

        def make_a(w, s):
            a_g[w, s] = keep.tile([P, T * N], BF16, name=f"ag_{w}{s}", align_bytes=64)
            a_c[w, s] = keep.tile([P, N], U32, name=f"ac_{w}{s}", align_bytes=64)
            a_s[w, s] = keep.tile([P, N], U8, name=f"as_{w}{s}", align_bytes=64)
            for tj in range(T):
                if s == "u":
                    factor = factor_cols(w, tj).rearrange("p i (b q) -> p b i q", q=4)
                else:
                    factor = ed[w][tj][:].rearrange("p (i b q) -> p b i q", i=T, q=4)
                nc.vector.tensor_tensor(
                    out=a_g[w, s][:, N * tj : N * (tj + 1)].rearrange("p (b q i) -> p b i q", q=4, i=T),
                    in0=g_sb[w, s][:].rearrange("p i (b q t) -> p t b i q", q=4, t=T)[:, tj, :, :, :],
                    in1=factor,
                    op=MULT,
                )

        def quant_a(w, s):
            for c0, c1 in HALVES:
                quant(a_c[w, s], a_s[w, s], a_g[w, s], c0, c1)

        m1 = {}

        def stage1(w, s):
            banks = []
            psum = {"0u": px, "0d": py, "1u": py, "1d": px}[f"{w}{s}"]
            for tm in range(T):
                bank = psum.tile([P, N], F32, name="bank")
                banks.append(bank)
            m1[w, s] = banks
            for tm in range(T):
                for tj in range(T):
                    nc.tensor.matmul_mx(
                        out=banks[tm][:, tj * P : (tj + 1) * P],
                        lhsT=a_c[w, s][:, tj * P : (tj + 1) * P].bitcast(FP8X4),
                        lhsT_scale=a_s[w, s][:, tj * P : (tj + 1) * P],
                        rhs=kf_c[:, tm * P : (tm + 1) * P].bitcast(FP8X4),
                        rhs_scale=kf_s[:, tm * P : (tm + 1) * P],
                        start=True,
                        stop=True,
                    )

        l_g, l_c, l_s = {}, {}, {}

        def copy_l(w, s):
            l_g[w, s] = keep.tile([P, T * N], BF16, name=f"lg_{w}{s}", align_bytes=64)
            for tm in range(T):
                nc.scalar.copy(
                    out=l_g[w, s][:, tm * N : (tm + 1) * N].rearrange("p (q t) -> p q t", t=T),
                    in_=m1[w, s][tm][:].rearrange("p (t q) -> p q t", t=T),
                )

        def quant_l(w, s):
            l_c[w, s] = keep.tile([P, N], U32, name=f"lc_{w}{s}", align_bytes=64)
            l_s[w, s] = keep.tile([P, N], U8, name=f"ls_{w}{s}", align_bytes=64)
            for c0, c1 in HALVES:
                quant(l_c[w, s], l_s[w, s], l_g[w, s], c0, c1)

        kb_g = keep.tile([P, T * N], BF16, name="kb_g", align_bytes=64)
        kb_c = keep.tile([P, N], U32, name="kb_c", align_bytes=64)
        kb_s = keep.tile([P, N], U8, name="kb_s", align_bytes=64)

        def copy_kb(h, copy):
            for tj in (2 * h, 2 * h + 1):
                copy(
                    out=kb_g[:, N * tj : N * (tj + 1)].rearrange("p (b q j) -> p b j q", q=4, j=T),
                    in_=kb_sb[:].rearrange("p j (b q t) -> p t b j q", q=4, t=T)[:, tj, :, :, :],
                )

        def quant_kb():
            for c0, c1 in HALVES:
                quant(kb_c, kb_s, kb_g, c0, c1)

        pu, pd = {}, {}

        def stage2_u(w):
            pu[w] = {}
            psum = (py, px)[w]
            for t2 in range(2):
                for far in range(2):
                    bank = psum.tile([P, N], F32, name="bank")
                    pu[w][t2, far] = bank
            for ti in range(T):
                for far in range(2):
                    half = (ti // 2) ^ far
                    cols = slice(2 * half * P, 2 * (half + 1) * P)
                    nc.tensor.matmul_mx(
                        out=pu[w][ti // 2, far][:, (ti % 2) * 2 * P : (ti % 2 + 1) * 2 * P],
                        lhsT=kb_c[:, ti * P : (ti + 1) * P].bitcast(FP8X4),
                        lhsT_scale=kb_s[:, ti * P : (ti + 1) * P],
                        rhs=l_c[w, "u"][:, cols].bitcast(FP8X4),
                        rhs_scale=l_s[w, "u"][:, cols],
                        start=True,
                        stop=True,
                    )

        def stage2_d(w):
            banks = []
            psum = (py, px)[w]
            for ti in range(T):
                bank = psum.tile([P, N], F32, name="bank")
                banks.append(bank)
                nc.tensor.matmul_mx(
                    out=bank[:],
                    lhsT=l_c[w, "d"][:, ti * P : (ti + 1) * P].bitcast(FP8X4),
                    lhsT_scale=l_s[w, "d"][:, ti * P : (ti + 1) * P],
                    rhs=kb_c[:].bitcast(FP8X4),
                    rhs_scale=kb_s[:],
                    start=True,
                    stop=True,
                )
            pd[w] = banks


        mask = keep.tile([P, 2, P, 2], F32, name="mask")
        nc.gpsimd.memset(mask[:], 0.0)
        for r in range(2):
            nc.gpsimd.tensor_copy(out=mask[:, r, :, r], in_=ident_f[:])

        n_sb = {}
        for w in range(W):
            part = keep.tile([P, T, N], F32, name=f"n_{w}")
            n_sb[w] = part

        def n_half(w, pair, half):
            return n_sb[w][:, 2 * pair : 2 * pair + 2, 2 * P * half : 2 * P * (half + 1)].rearrange(
                "p r (q t) -> p r q t", t=2
            )

        def minus_pu(w):
            for pair in range(2):
                nc.scalar.mul(
                    out=n_half(w, pair, 1 - pair),
                    in_=pu[w][pair, 1][:].rearrange("p (r t q) -> p r q t", r=2, t=2),
                    mul=-1.0,
                )

        def diag_pu(w):
            for pair in range(2):
                nc.vector.tensor_tensor(
                    out=n_half(w, pair, pair),
                    in0=mask[:],
                    in1=pu[w][pair, 0][:].rearrange("p (r t q) -> p r q t", r=2, t=2),
                    op=SUB,
                )

        o_sb, o_g = {}, {}
        w_c = keep.tile([P, W * N], U32, name="w_c", align_bytes=64)
        w_s = keep.tile([P, W * N], U8, name="w_s", align_bytes=64)

        def product(w, h):
            if h == 0:
                o_g[w] = keep.tile([P, T * N], BF16, name=f"og_{w}", align_bytes=64)
            dst = out_0[w].rearrange("(p t) n -> p t n", t=T)
            cols = slice(256 * h, 256 * (h + 1))
            o_sb[w, h] = keep.tile([P, T, 256], F32, name=f"o_{w}{h}")
            qs = slice(64 * h, 64 * (h + 1))
            for ti in range(T):
                nc.vector.tensor_tensor(
                    out=o_sb[w, h][:, ti, :].rearrange("p (q a b) -> p q a b", a=2, b=2),
                    in0=pd[w][ti][:].rearrange("p (a b q) -> p q a b", a=2, b=2)[:, qs, :, :],
                    in1=n_sb[w][:, ti, :].rearrange("p (a q b) -> p q a b", a=2, b=2)[:, qs, :, :],
                    op=MULT,
                )
            nc.sync.dma_start(out=dst[:, :, cols], in_=o_sb[w, h][:])

        def planes_copy(w, h, copy, c0=0, c1=256):
            copy(
                out=o_g[w][:, 1024 * h + T * c0 : 1024 * h + T * c1].rearrange("p (b n t) -> p b t n", n=4, t=T),
                in_=o_sb[w, h][:, :, c0:c1].rearrange("p t (b n) -> p b t n", n=4),
            )

        def planes_quant(w, h):
            cols = slice(w * N + 256 * h, w * N + 256 * (h + 1))
            nc.vector.quantize_mx(
                out=w_c[:, cols].bitcast(FP8X4),
                scales=w_s[:, cols],
                in_=o_g[w][:, 1024 * h : 1024 * (h + 1)],
            )

        def store_words(c0, c1):
            nc.sync.dma_start(
                out=out_1[0].rearrange("p m t -> p (m t)").bitcast(I32)[:, c0:c1],
                in_=w_c[:, c0:c1].bitcast(I32),
            )

        vcopy, scopy = nc.vector.tensor_copy, nc.scalar.copy
        spread_v(0)
        turn_kf()
        factors(0, 4)
        copy_kf(0, scopy)
        copy_kf(1, scopy)
        make_a(0, "u")
        spread_v(1)
        turn_factors(0)
        quant_a(0, "u")
        quant_kf()
        factors(1, 1)
        stage1(0, "u")
        make_a(0, "d")
        copy_kb(0, scopy)
        copy_kb(1, scopy)
        quant_a(0, "d")
        stage1(0, "d")
        copy_l(0, "u")
        turn_factors(1)
        make_a(1, "u")
        quant_a(1, "u")
        copy_l(0, "d")
        stage1(1, "u")
        make_a(1, "d")
        quant_a(1, "d")
        copy_l(1, "u")
        stage1(1, "d")
        quant_kb()
        quant_l(0, "u")
        stage2_u(0)
        quant_l(0, "d")
        stage2_d(0)
        minus_pu(0)
        copy_l(1, "d")
        quant_l(1, "u")
        stage2_u(1)
        diag_pu(0)
        product(0, 0)
        product(0, 1)
        quant_l(1, "d")
        stage2_d(1)
        diag_pu(1)
        minus_pu(1)
        planes_copy(0, 0, scopy)
        planes_copy(0, 1, scopy)
        product(1, 0)
        planes_quant(0, 0)
        product(1, 1)
        planes_copy(1, 0, scopy)
        planes_quant(0, 1)
        store_words(0, 512)
        planes_copy(1, 1, vcopy, 0, 160)
        planes_copy(1, 1, scopy, 160, 256)
        planes_quant(1, 0)
        store_words(512, 768)
        planes_quant(1, 1)
        store_words(768, 1024)
        for quad in range(4):
            queue = nc.scalar if quad < 2 else nc.sync
            queue.dma_start(
                out=out_2[0].bitcast(I32)[4 * quad : 4 * quad + 4, :],
                in_=w_s[32 * quad : 32 * quad + 4, :].bitcast(I32),
            )
